import numpy as np
import ml_dtypes


def mxq(x, axis, fmt="e4m3"):
    dtype, down = {"e4m3": (ml_dtypes.float8_e4m3fn, 7), "e5m2": (ml_dtypes.float8_e5m2, 14)}[fmt]
    v = np.moveaxis(np.asarray(x, np.float32).astype(ml_dtypes.bfloat16).astype(np.float64), axis, -1)
    blocks = v.reshape(v.shape[:-1] + (-1, 32))
    amax = np.abs(blocks).max(-1, keepdims=True)
    byte = np.maximum(np.where(amax > 0, np.frexp(amax)[1] - 1 + 127, 0) - down, 1)
    scale = np.exp2(byte - 127.0)
    codes = (blocks / scale).astype(np.float32).astype(dtype).astype(np.float64)
    return np.moveaxis((codes * scale).reshape(v.shape), -1, axis)


WIDE = False


def mx_kscale(k):
    if not WIDE:
        return np.ones(k)
    levels = np.array([10, -10, 5, -5, 0])
    if k % 512:
        return np.exp2(np.random.permutation(np.resize(levels, k // 32))).repeat(32)
    a = np.empty((k // 512, 16))
    for p in range(k // 512):
        a[p, :8] = np.random.permutation(np.resize(levels, 8))
        for g in range(8):
            far = levels[np.abs(levels - a[p, g]) >= 10]
            a[p, g + 8] = far[np.random.randint(len(far))]
    return np.exp2(a.ravel()).repeat(32)


def f64(x):
    return np.asarray(x).astype(np.float64)


def striped8(idx):
    return np.asarray(idx).reshape(8, -1, 16).transpose(0, 2, 1).reshape(128, -1).astype(np.uint16)


def unstriped8(offs):
    return offs.reshape(8, 16, -1).transpose(0, 2, 1).reshape(8, -1).astype(np.int64)


def pick8(x, idx, run):
    r = np.arange(len(x))
    return x[r[:, None], idx[r % (8 * run) // run]]


E2M1 = np.array([0.0, 0.5, 1.0, 1.5, 2.0, 3.0, 4.0, 6.0, -0.0, -0.5, -1.0, -1.5, -2.0, -3.0, -4.0, -6.0])


def pack_weight(w, fmt):
    k, n = w.shape
    w = f64(np.asarray(w, np.float32).astype(ml_dtypes.bfloat16)).reshape(k // 32, 32, n)
    amax = np.abs(w).max(1)
    if fmt == "e4m3":
        byte = np.frexp(amax)[1] - 1 + 127 - 7
    else:
        mant, ex = np.frexp(amax / 6.0)
        byte = np.where(mant > 0.5, ex, ex - 1) + 127
    byte = np.clip(np.where(amax > 0, byte, 1), 1, 254)
    scaled = (w * np.exp2(127.0 - byte)[:, None, :]).reshape(k, n).astype(np.float32)
    by_word = np.ascontiguousarray(scaled.reshape(k // 512, 128, 4, n).transpose(0, 1, 3, 2))
    if fmt == "e4m3":
        words = by_word.astype(ml_dtypes.float8_e4m3fn).view(np.uint8)
    else:
        c = by_word.astype(ml_dtypes.float4_e2m1fn).view(np.uint8) & 0xF
        words = (c[..., 0::2] | (c[..., 1::2] << 4)).reshape(k // 512, 128, 2 * n)
    return np.ascontiguousarray(words), np.ascontiguousarray(byte.astype(np.uint8).reshape(k // 512, 16, n))


def unpack_weight(words, scales, fmt):
    g, _, n = scales.shape
    words = np.ascontiguousarray(words).reshape(g, 128, n, -1)
    if fmt == "e4m3":
        vals = words.view(ml_dtypes.float8_e4m3fn).astype(np.float64)
    else:
        nib = np.empty((g, 128, n, 4), np.uint8)
        nib[..., 0::2] = words & 0xF
        nib[..., 1::2] = words >> 4
        vals = E2M1[nib]
    vals = vals * np.repeat(np.exp2(scales.astype(np.float64) - 127.0), 8, axis=1)[..., None]
    return vals.transpose(0, 1, 3, 2).reshape(g * 512, n)


D, T, I, Q = 512, 1024, 512, 128


def setup_inputs():
    n = np.random.standard_normal
    idx = np.stack([np.random.permutation(T)[:I] for _ in range(8)])
    idx2 = np.stack([np.random.permutation(T)[:I] for _ in range(8)])
    idx3 = np.stack([np.random.permutation(T)[:I] for _ in range(8)])
    fd = mx_kscale(D)
    keysp = pack_weight(n((D, T)) / fd[:, None], "e4m3")
    return {
        "query": (n((D, Q)) * 1.0 / np.sqrt(D) * fd[:, None]).astype(np.float32),
        "keys_words": keysp[0],
        "keys_scales": keysp[1],
        "old": (1.0 * n((Q, T))).astype(np.float32),
        "share2": (np.random.uniform(0.4, 1.2, (Q, 1))).astype(np.float32),
        "offs": striped8(idx),
        "offs2": striped8(idx2),
        "offs3": striped8(idx3),
    }


def reference(query, keys_words, keys_scales, old, share2, offs, offs2, offs3):
    idx = unstriped8(offs)
    idx2 = unstriped8(offs2)
    idx3 = unstriped8(offs3)
    keysu = unpack_weight(keys_words, keys_scales, "e4m3")
    queryq = mxq(f64(query), 0, "e4m3")
    a = queryq.T @ keysu
    s = pick8(a, idx, 16) - pick8(a, idx2, 16)
    w = np.maximum(s, 0.0)
    f1 = np.zeros((Q, T))
    f1[np.arange(Q)[:, None], idx[np.arange(Q) % 128 // 16]] = w
    f2 = np.zeros((Q, T))
    f2[np.arange(Q)[:, None], idx3[np.arange(Q) % 128 // 16]] = w
    y = f64(old) + f1 + f2 * f64(share2)
    return y

@@ -1,0 +1,143 @@
+from contextlib import ExitStack
+
+import concourse.mybir as mybir
+from concourse.masks import make_identity
+
+D, T, I, Q = 512, 1024, 512, 128
+FLOPS = 2 * D * T * Q
+
+F32 = mybir.dt.float32
+BF16 = mybir.dt.bfloat16
+I32 = mybir.dt.int32
+U32 = mybir.dt.uint32
+U16 = mybir.dt.uint16
+U8 = mybir.dt.uint8
+FP8X4 = mybir.dt.float8_e4m3fn_x4
+MULT = mybir.AluOpType.mult
+ADD = mybir.AluOpType.add
+MAX = mybir.AluOpType.max
+COPY = mybir.ActivationFunctionType.Copy
+
+P = 128
+PACK = 4
+BANK = 512
+N_MX = 256
+HALF = I // 2
+STORE = 256
+
+
+def tile_attend_difference_lean_twiceput_heads_kernel(tc, query, keys_words, keys_scales, old, share2, offs, offs2, offs3, out):
+    nc = tc.nc
+    with ExitStack() as ctx:
+        sb = ctx.enter_context(tc.tile_pool(name="sb", bufs=1))
+        ps = ctx.enter_context(tc.psum_pool(name="ps", bufs=1))
+
+        list1 = sb.tile([P, I // 16], U16, name="list1")
+        list2 = sb.tile([P, I // 16], U16, name="list2")
+        list3 = sb.tile([P, I // 16], U16, name="list3")
+        q_raw = sb.tile([P, PACK, Q], F32, name="q_raw")
+        q_bf = sb.tile([P, Q, PACK], BF16, name="q_bf", align_bytes=64)
+        q_codes = sb.tile([P, Q], U32, name="q_codes", align_bytes=64)
+        q_scales = sb.tile([P, Q], U8, name="q_scales", align_bytes=64)
+        k_codes = sb.tile([P, T], I32, name="k_codes", align_bytes=64)
+        k_scales = sb.tile([P, T], U8, name="k_scales", align_bytes=64)
+        old_sb = sb.tile([P, T], F32, name="old_sb")
+        share_sb = sb.tile([P, 1], F32, name="share_sb")
+        ident = sb.tile([P, P], F32, name="ident")
+        a = sb.tile([P, T], F32, name="a")
+        g1 = sb.tile([P, I], F32, name="g1")
+        ng2 = sb.tile([P, I], F32, name="ng2")
+        top = sb.tile([P, I], F32, name="top")
+        f1 = sb.tile([P, T], F32, name="f1")
+        f2 = sb.tile([P, T], F32, name="f2")
+        turned = sb.tile([P, T], F32, name="turned")
+        res = sb.tile([P, T], F32, name="res")
+
+        nc.vector.memset(k_scales[:].bitcast(I32), 0)
+        nc.sync.dma_start(out=q_raw[:], in_=query.rearrange("(p j) q -> p j q", j=PACK))
+        nc.sync.dma_start(out=k_codes[:], in_=keys_words[0].rearrange("p n t -> p (n t)").bitcast(I32))
+        for quad in range(4):
+            nc.scalar.dma_start(
+                out=k_scales[32 * quad : 32 * quad + 4, :].bitcast(I32),
+                in_=keys_scales[0][4 * quad : 4 * quad + 4, :].bitcast(I32),
+            )
+        nc.sync.dma_start(list2[:], offs2)
+        nc.sync.dma_start(list1[:], offs)
+        nc.sync.dma_start(list3[:], offs3)
+        nc.sync.dma_start(out=old_sb[:], in_=old)
+        nc.sync.dma_start(out=share_sb[:], in_=share2)
+
+        nc.vector.memset(f1[:], 0.0)
+        nc.vector.memset(f2[:], 0.0)
+        make_identity(nc, ident[:])
+
+        nc.vector.tensor_copy(out=q_bf[:], in_=q_raw[:].rearrange("p j q -> p q j"))
+        nc.vector.quantize_mx(out=q_codes[:].bitcast(FP8X4), scales=q_scales[:], in_=q_bf[:].rearrange("p q j -> p (q j)"))
+
+        for c in range(T // N_MX):
+            cols = slice(c * N_MX, (c + 1) * N_MX)
+            acc = ps.tile([P, N_MX], F32, name=f"acc{c}")
+            nc.tensor.matmul_mx(
+                out=acc[:],
+                lhsT=q_codes[:].bitcast(FP8X4),
+                lhsT_scale=q_scales[:],
+                rhs=k_codes[:, cols].bitcast(FP8X4),
+                rhs_scale=k_scales[:, cols],
+                start=True,
+                stop=True,
+            )
+            if c % 2 == 0:
+                nc.scalar.activation(a[:, cols], acc[:], COPY)
+            else:
+                nc.vector.tensor_copy(out=a[:, cols], in_=acc[:])
+
+        down = [ps.tile([P, BANK], F32, name=f"down{b}") for b in range(T // BANK)]
+        back = [ps.tile([P, BANK], F32, name=f"back{b}") for b in range(T // BANK)]
+        per_bank = BANK // P
+        for b in range(T // BANK):
+            for j in range(per_bank):
+                nc.tensor.matmul(
+                    down[b][:, j * P : (j + 1) * P],
+                    lhsT=old_sb[:, b * BANK + j * P : b * BANK + (j + 1) * P],
+                    rhs=ident[:],
+                    is_transpose=True,
+                    start=(j == 0),
+                    stop=False,
+                )
+
+        s0, s1 = slice(0, HALF), slice(HALF, I)
+        l0, l1 = slice(0, HALF // 16), slice(HALF // 16, I // 16)
+        nc.scalar.activation(ng2[:, s0], a[:].indirect(list2[:, l0]), COPY, scale=-1.0)
+        nc.vector.tensor_copy(g1[:, s0], a[:].indirect(list1[:, l0]))
+        nc.scalar.activation(ng2[:, s1], a[:].indirect(list2[:, l1]), COPY, scale=-1.0)
+        nc.scalar.activation(g1[:, s1], a[:].indirect(list1[:, l1]), COPY)
+        for s, l in ((s0, l0), (s1, l1)):
+            nc.vector.scalar_tensor_tensor(top[:, s], ng2[:, s], -1.0, g1[:, s], MULT, MAX)
+            nc.vector.tensor_tensor(f1[:].indirect(list1[:, l]), top[:, s], ng2[:, s], ADD)
+        nc.vector.tensor_tensor(f2[:].indirect(list3[:]), top[:], ng2[:], ADD)
+
+        for b in range(T // BANK):
+            for j in range(per_bank):
+                nc.tensor.matmul(
+                    down[b][:, j * P : (j + 1) * P],
+                    lhsT=f1[:, b * BANK + j * P : b * BANK + (j + 1) * P],
+                    rhs=ident[:],
+                    is_transpose=True,
+                    start=False,
+                    stop=(j == per_bank - 1),
+                )
+            nc.scalar.copy(turned[:, b * BANK : (b + 1) * BANK], down[b][:])
+        for b in range(T // BANK):
+            for j in range(per_bank):
+                nc.tensor.transpose(
+                    back[b][:, j * P : (j + 1) * P],
+                    turned[:, b * BANK + j * P : b * BANK + (j + 1) * P],
+                    ident[:],
+                )
+
+        for c in range(T // STORE):
+            cols = slice(c * STORE, (c + 1) * STORE)
+            b, off = divmod(c * STORE, BANK)
+            nc.vector.scalar_tensor_tensor(res[:, cols], f2[:, cols], share_sb[:, 0:1], back[b][:, off : off + STORE], MULT, ADD)
+            queue = nc.sync if c % 2 == 0 else nc.scalar
+            queue.dma_start(out=out[:, cols], in_=res[:, cols])

@@ -39,7 +39,7 @@ def tile_attend_difference_lean_twiceput_heads_kernel(tc, query, keys_words, key
         q_bf = sb.tile([P, Q, PACK], BF16, name="q_bf", align_bytes=64)
         q_codes = sb.tile([P, Q], U32, name="q_codes", align_bytes=64)
         q_scales = sb.tile([P, Q], U8, name="q_scales", align_bytes=64)
-        k_codes = sb.tile([P, T], I32, name="k_codes", align_bytes=64)
+        k_codes = [sb.tile([P, BANK], I32, name=f"k_codes{h}", align_bytes=64) for h in range(T // BANK)]
         k_scales = sb.tile([P, T], U8, name="k_scales", align_bytes=64)
         old_sb = sb.tile([P, T], F32, name="old_sb")
         share_sb = sb.tile([P, 1], F32, name="share_sb")
@@ -53,9 +53,11 @@ def tile_attend_difference_lean_twiceput_heads_kernel(tc, query, keys_words, key
         turned = sb.tile([P, T], F32, name="turned")
         res = sb.tile([P, T], F32, name="res")
 
-        nc.vector.memset(k_scales[:].bitcast(I32), 0)
+        nc.gpsimd.memset(k_scales[:].bitcast(I32), 0)
         nc.sync.dma_start(out=q_raw[:], in_=query.rearrange("(p j) q -> p j q", j=PACK))
-        nc.sync.dma_start(out=k_codes[:], in_=keys_words[0].rearrange("p n t -> p (n t)").bitcast(I32))
+        key_words = keys_words[0].rearrange("p n t -> p (n t)").bitcast(I32)
+        for h in range(T // BANK):
+            nc.sync.dma_start(out=k_codes[h][:], in_=key_words[:, h * BANK : (h + 1) * BANK])
         for quad in range(4):
             nc.scalar.dma_start(
                 out=k_scales[32 * quad : 32 * quad + 4, :].bitcast(I32),
@@ -71,17 +73,25 @@ def tile_attend_difference_lean_twiceput_heads_kernel(tc, query, keys_words, key
         nc.vector.memset(f2[:], 0.0)
         make_identity(nc, ident[:])
 
-        nc.vector.tensor_copy(out=q_bf[:], in_=q_raw[:].rearrange("p j q -> p q j"))
-        nc.vector.quantize_mx(out=q_codes[:].bitcast(FP8X4), scales=q_scales[:], in_=q_bf[:].rearrange("p q j -> p (q j)"))
+        q_halves = (slice(0, Q // 2), slice(Q // 2, Q))
+        for rows in q_halves:
+            nc.vector.tensor_copy(out=q_bf[:, rows, :], in_=q_raw[:, :, rows].rearrange("p j q -> p q j"))
+        for rows in q_halves:
+            nc.vector.quantize_mx(
+                out=q_codes[:, rows].bitcast(FP8X4),
+                scales=q_scales[:, rows],
+                in_=q_bf[:, rows, :].rearrange("p q j -> p (q j)"),
+            )
 
         for c in range(T // N_MX):
             cols = slice(c * N_MX, (c + 1) * N_MX)
+            h, off = divmod(c * N_MX, BANK)
             acc = ps.tile([P, N_MX], F32, name=f"acc{c}")
             nc.tensor.matmul_mx(
                 out=acc[:],
                 lhsT=q_codes[:].bitcast(FP8X4),
                 lhsT_scale=q_scales[:],
-                rhs=k_codes[:, cols].bitcast(FP8X4),
+                rhs=k_codes[h][:, off : off + N_MX].bitcast(FP8X4),
                 rhs_scale=k_scales[:, cols],
                 start=True,
                 stop=True,

@@ -40,7 +40,7 @@ def tile_attend_difference_lean_twiceput_heads_kernel(tc, query, keys_words, key
         q_codes = sb.tile([P, Q], U32, name="q_codes", align_bytes=64)
         q_scales = sb.tile([P, Q], U8, name="q_scales", align_bytes=64)
         k_codes = [sb.tile([P, BANK], I32, name=f"k_codes{h}", align_bytes=64) for h in range(T // BANK)]
-        k_scales = sb.tile([P, T], U8, name="k_scales", align_bytes=64)
+        k_scales = sb.tile([P, N_MX], U8, name="k_scales", align_bytes=64)
         old_sb = sb.tile([P, T], F32, name="old_sb")
         share_sb = sb.tile([P, 1], F32, name="share_sb")
         ident = sb.tile([P, P], F32, name="ident")
@@ -53,16 +53,17 @@ def tile_attend_difference_lean_twiceput_heads_kernel(tc, query, keys_words, key
         turned = sb.tile([P, T], F32, name="turned")
         res = sb.tile([P, T], F32, name="res")
 
-        nc.gpsimd.memset(k_scales[:].bitcast(I32), 0)
+        nc.vector.memset(k_scales[:].bitcast(I32), 0)
         nc.sync.dma_start(out=q_raw[:], in_=query.rearrange("(p j) q -> p j q", j=PACK))
+        scale_words = keys_scales[0].bitcast(I32)
+        for quad in range(4):
+            nc.sync.dma_start(
+                out=k_scales[32 * quad : 32 * quad + 16, :].bitcast(I32),
+                in_=scale_words[4 * quad : 4 * quad + 4, :].rearrange("r (c w) -> c r w", c=T // N_MX),
+            )
         key_words = keys_words[0].rearrange("p n t -> p (n t)").bitcast(I32)
         for h in range(T // BANK):
             nc.sync.dma_start(out=k_codes[h][:], in_=key_words[:, h * BANK : (h + 1) * BANK])
-        for quad in range(4):
-            nc.scalar.dma_start(
-                out=k_scales[32 * quad : 32 * quad + 4, :].bitcast(I32),
-                in_=keys_scales[0][4 * quad : 4 * quad + 4, :].bitcast(I32),
-            )
         nc.sync.dma_start(list2[:], offs2)
         nc.sync.dma_start(list1[:], offs)
         nc.sync.dma_start(list3[:], offs3)
@@ -92,7 +93,7 @@ def tile_attend_difference_lean_twiceput_heads_kernel(tc, query, keys_words, key
                 lhsT=q_codes[:].bitcast(FP8X4),
                 lhsT_scale=q_scales[:],
                 rhs=k_codes[h][:, off : off + N_MX].bitcast(FP8X4),
-                rhs_scale=k_scales[:, cols],
+                rhs_scale=k_scales[4 * c :, :],
                 start=True,
                 stop=True,
             )
@@ -101,14 +102,14 @@ def tile_attend_difference_lean_twiceput_heads_kernel(tc, query, keys_words, key
             else:
                 nc.vector.tensor_copy(out=a[:, cols], in_=acc[:])
 
-        down = [ps.tile([P, BANK], F32, name=f"down{b}") for b in range(T // BANK)]
-        back = [ps.tile([P, BANK], F32, name=f"back{b}") for b in range(T // BANK)]
-        per_bank = BANK // P
-        for b in range(T // BANK):
-            for j in range(per_bank):
+        n_part = T // N_MX
+        per_part = N_MX // P
+        down = [ps.tile([P, N_MX], F32, name=f"down{b}") for b in range(n_part)]
+        for b in range(n_part):
+            for j in range(per_part):
                 nc.tensor.matmul(
                     down[b][:, j * P : (j + 1) * P],
-                    lhsT=old_sb[:, b * BANK + j * P : b * BANK + (j + 1) * P],
+                    lhsT=old_sb[:, b * N_MX + j * P : b * N_MX + (j + 1) * P],
                     rhs=ident[:],
                     is_transpose=True,
                     start=(j == 0),
@@ -126,28 +127,36 @@ def tile_attend_difference_lean_twiceput_heads_kernel(tc, query, keys_words, key
             nc.vector.tensor_tensor(f1[:].indirect(list1[:, l]), top[:, s], ng2[:, s], ADD)
         nc.vector.tensor_tensor(f2[:].indirect(list3[:]), top[:], ng2[:], ADD)
 
-        for b in range(T // BANK):
-            for j in range(per_bank):
+        back = [ps.tile([P, N_MX], F32, name=f"acc{b}") for b in range(n_part)]
+
+        def turn_down(b):
+            for j in range(per_part):
                 nc.tensor.matmul(
                     down[b][:, j * P : (j + 1) * P],
-                    lhsT=f1[:, b * BANK + j * P : b * BANK + (j + 1) * P],
+                    lhsT=f1[:, b * N_MX + j * P : b * N_MX + (j + 1) * P],
                     rhs=ident[:],
                     is_transpose=True,
                     start=False,
-                    stop=(j == per_bank - 1),
+                    stop=(j == per_part - 1),
                 )
-            nc.scalar.copy(turned[:, b * BANK : (b + 1) * BANK], down[b][:])
-        for b in range(T // BANK):
-            for j in range(per_bank):
+            nc.scalar.copy(turned[:, b * N_MX : (b + 1) * N_MX], down[b][:])
+
+        def turn_back(b):
+            for j in range(per_part):
                 nc.tensor.transpose(
                     back[b][:, j * P : (j + 1) * P],
-                    turned[:, b * BANK + j * P : b * BANK + (j + 1) * P],
+                    turned[:, b * N_MX + j * P : b * N_MX + (j + 1) * P],
                     ident[:],
                 )
 
-        for c in range(T // STORE):
-            cols = slice(c * STORE, (c + 1) * STORE)
-            b, off = divmod(c * STORE, BANK)
-            nc.vector.scalar_tensor_tensor(res[:, cols], f2[:, cols], share_sb[:, 0:1], back[b][:, off : off + STORE], MULT, ADD)
+        for b in range(n_part + 2):
+            if b < n_part:
+                turn_down(b)
+            if b >= 2:
+                turn_back(b - 2)
+
+        for c in range(n_part):
+            cols = slice(c * N_MX, (c + 1) * N_MX)
+            nc.vector.scalar_tensor_tensor(res[:, cols], f2[:, cols], share_sb[:, 0:1], back[c][:], MULT, ADD)
             queue = nc.sync if c % 2 == 0 else nc.scalar
             queue.dma_start(out=out[:, cols], in_=res[:, cols])

@@ -36,7 +36,7 @@ def tile_attend_difference_lean_twiceput_heads_kernel(tc, query, keys_words, key
         list2 = sb.tile([P, I // 16], U16, name="list2")
         list3 = sb.tile([P, I // 16], U16, name="list3")
         q_raw = sb.tile([P, PACK, Q], F32, name="q_raw")
-        q_bf = sb.tile([P, Q, PACK], BF16, name="q_bf", align_bytes=64)
+        q_bf = sb.tile([P, Q, PACK], BF16, name="q_bf", tag="q_bf_then_f2", align_bytes=64)
         q_codes = sb.tile([P, Q], U32, name="q_codes", align_bytes=64)
         q_scales = sb.tile([P, Q], U8, name="q_scales", align_bytes=64)
         k_codes = [sb.tile([P, BANK], I32, name=f"k_codes{h}", align_bytes=64) for h in range(T // BANK)]
@@ -48,8 +48,7 @@ def tile_attend_difference_lean_twiceput_heads_kernel(tc, query, keys_words, key
         g1 = sb.tile([P, I], F32, name="g1")
         ng2 = sb.tile([P, I], F32, name="ng2")
         top = sb.tile([P, I], F32, name="top")
-        f1 = sb.tile([P, T], F32, name="f1")
-        f2 = sb.tile([P, T], F32, name="f2")
+        f1 = [sb.tile([P, T], F32, name=f"f1_{h}") for h in range(2)]
         turned = sb.tile([P, T], F32, name="turned")
         res = sb.tile([P, T], F32, name="res")
 
@@ -70,8 +69,8 @@ def tile_attend_difference_lean_twiceput_heads_kernel(tc, query, keys_words, key
         nc.sync.dma_start(out=old_sb[:], in_=old)
         nc.sync.dma_start(out=share_sb[:], in_=share2)
 
-        nc.vector.memset(f1[:], 0.0)
-        nc.vector.memset(f2[:], 0.0)
+        for h in range(2):
+            nc.vector.memset(f1[h][:], 0.0)
         make_identity(nc, ident[:])
 
         q_halves = (slice(0, Q // 2), slice(Q // 2, Q))
@@ -83,6 +82,9 @@ def tile_attend_difference_lean_twiceput_heads_kernel(tc, query, keys_words, key
                 scales=q_scales[:, rows],
                 in_=q_bf[:, rows, :].rearrange("p q j -> p (q j)"),
             )
+
+        f2 = sb.tile([P, T], F32, name="f2", tag="q_bf_then_f2", align_bytes=64)
+        nc.vector.memset(f2[:], 0.0)
 
         for c in range(T // N_MX):
             cols = slice(c * N_MX, (c + 1) * N_MX)
@@ -118,14 +120,26 @@ def tile_attend_difference_lean_twiceput_heads_kernel(tc, query, keys_words, key
 
         s0, s1 = slice(0, HALF), slice(HALF, I)
         l0, l1 = slice(0, HALF // 16), slice(HALF // 16, I // 16)
-        nc.scalar.activation(ng2[:, s0], a[:].indirect(list2[:, l0]), COPY, scale=-1.0)
-        nc.vector.tensor_copy(g1[:, s0], a[:].indirect(list1[:, l0]))
-        nc.scalar.activation(ng2[:, s1], a[:].indirect(list2[:, l1]), COPY, scale=-1.0)
-        nc.scalar.activation(g1[:, s1], a[:].indirect(list1[:, l1]), COPY)
-        for s, l in ((s0, l0), (s1, l1)):
+        halves = ((s0, l0), (s1, l1))
+        for s, l in halves:
+            nc.scalar.activation(ng2[:, s], a[:].indirect(list2[:, l]), COPY, scale=-1.0)
+            nc.vector.tensor_copy(g1[:, s], a[:].indirect(list1[:, l]))
+        for s, l in halves:
             nc.vector.scalar_tensor_tensor(top[:, s], ng2[:, s], -1.0, g1[:, s], MULT, MAX)
-            nc.vector.tensor_tensor(f1[:].indirect(list1[:, l]), top[:, s], ng2[:, s], ADD)
+        for h, (s, l) in enumerate(halves):
+            nc.vector.tensor_tensor(f1[h][:].indirect(list1[:, l]), top[:, s], ng2[:, s], ADD)
         nc.vector.tensor_tensor(f2[:].indirect(list3[:]), top[:], ng2[:], ADD)
+
+        for b in range(n_part):
+            for j in range(per_part):
+                nc.tensor.matmul(
+                    down[b][:, j * P : (j + 1) * P],
+                    lhsT=f1[0][:, b * N_MX + j * P : b * N_MX + (j + 1) * P],
+                    rhs=ident[:],
+                    is_transpose=True,
+                    start=False,
+                    stop=False,
+                )
 
         back = [ps.tile([P, N_MX], F32, name=f"acc{b}") for b in range(n_part)]
 
@@ -133,7 +147,7 @@ def tile_attend_difference_lean_twiceput_heads_kernel(tc, query, keys_words, key
             for j in range(per_part):
                 nc.tensor.matmul(
                     down[b][:, j * P : (j + 1) * P],
-                    lhsT=f1[:, b * N_MX + j * P : b * N_MX + (j + 1) * P],
+                    lhsT=f1[1][:, b * N_MX + j * P : b * N_MX + (j + 1) * P],
                     rhs=ident[:],
                     is_transpose=True,
                     start=False,

from contextlib import ExitStack

import concourse.mybir as mybir
from concourse.masks import make_identity

D, T, I, Q = 512, 1024, 512, 128
FLOPS = 2 * D * T * Q

F32 = mybir.dt.float32
BF16 = mybir.dt.bfloat16
I32 = mybir.dt.int32
U32 = mybir.dt.uint32
U16 = mybir.dt.uint16
U8 = mybir.dt.uint8
FP8X4 = mybir.dt.float8_e4m3fn_x4
MULT = mybir.AluOpType.mult
ADD = mybir.AluOpType.add
MAX = mybir.AluOpType.max
COPY = mybir.ActivationFunctionType.Copy

P = 128
PACK = 4
BANK = 512
N_MX = 256
HALF = I // 2
STORE = 256


def tile_attend_difference_lean_twiceput_heads_kernel(tc, query, keys_words, keys_scales, old, share2, offs, offs2, offs3, out):
    nc = tc.nc
    with ExitStack() as ctx:
        sb = ctx.enter_context(tc.tile_pool(name="sb", bufs=1))
        ps = ctx.enter_context(tc.psum_pool(name="ps", bufs=1))

        list1 = sb.tile([P, I // 16], U16, name="list1")
        list2 = sb.tile([P, I // 16], U16, name="list2")
        list3 = sb.tile([P, I // 16], U16, name="list3")
        q_raw = sb.tile([P, PACK, Q], F32, name="q_raw")
        q_bf = sb.tile([P, Q, PACK], BF16, name="q_bf", tag="q_bf_then_f2", align_bytes=64)
        q_codes = sb.tile([P, Q], U32, name="q_codes", align_bytes=64)
        q_scales = sb.tile([P, Q], U8, name="q_scales", align_bytes=64)
        k_codes = [sb.tile([P, BANK], I32, name=f"k_codes{h}", align_bytes=64) for h in range(T // BANK)]
        k_scales = sb.tile([P, N_MX], U8, name="k_scales", align_bytes=64)
        old_sb = sb.tile([P, T], F32, name="old_sb")
        share_sb = sb.tile([P, 1], F32, name="share_sb")
        ident = sb.tile([P, P], F32, name="ident")
        a = sb.tile([P, T], F32, name="a")
        g1 = sb.tile([P, I], F32, name="g1")
        ng2 = sb.tile([P, I], F32, name="ng2")
        top = sb.tile([P, I], F32, name="top")
        f1 = [sb.tile([P, T], F32, name=f"f1_{h}") for h in range(2)]
        turned = sb.tile([P, T], F32, name="turned")
        res = sb.tile([P, T], F32, name="res")

        nc.vector.memset(k_scales[:].bitcast(I32), 0)
        nc.sync.dma_start(out=q_raw[:], in_=query.rearrange("(p j) q -> p j q", j=PACK))
        scale_words = keys_scales[0].bitcast(I32)
        for quad in range(4):
            nc.sync.dma_start(
                out=k_scales[32 * quad : 32 * quad + 16, :].bitcast(I32),
                in_=scale_words[4 * quad : 4 * quad + 4, :].rearrange("r (c w) -> c r w", c=T // N_MX),
            )
        key_words = keys_words[0].rearrange("p n t -> p (n t)").bitcast(I32)
        for h in range(T // BANK):
            nc.sync.dma_start(out=k_codes[h][:], in_=key_words[:, h * BANK : (h + 1) * BANK])
        nc.sync.dma_start(list2[:], offs2)
        nc.sync.dma_start(list1[:], offs)
        nc.sync.dma_start(list3[:], offs3)
        nc.sync.dma_start(out=old_sb[:], in_=old)
        nc.sync.dma_start(out=share_sb[:], in_=share2)

        for h in range(2):
            nc.vector.memset(f1[h][:], 0.0)
        make_identity(nc, ident[:])

        q_halves = (slice(0, Q // 2), slice(Q // 2, Q))
        for rows in q_halves:
            nc.vector.tensor_copy(out=q_bf[:, rows, :], in_=q_raw[:, :, rows].rearrange("p j q -> p q j"))
        for rows in q_halves:
            nc.vector.quantize_mx(
                out=q_codes[:, rows].bitcast(FP8X4),
                scales=q_scales[:, rows],
                in_=q_bf[:, rows, :].rearrange("p q j -> p (q j)"),
            )

        f2 = sb.tile([P, T], F32, name="f2", tag="q_bf_then_f2", align_bytes=64)
        nc.vector.memset(f2[:], 0.0)

        for c in range(T // N_MX):
            cols = slice(c * N_MX, (c + 1) * N_MX)
            h, off = divmod(c * N_MX, BANK)
            acc = ps.tile([P, N_MX], F32, name=f"acc{c}")
            nc.tensor.matmul_mx(
                out=acc[:],
                lhsT=q_codes[:].bitcast(FP8X4),
                lhsT_scale=q_scales[:],
                rhs=k_codes[h][:, off : off + N_MX].bitcast(FP8X4),
                rhs_scale=k_scales[4 * c :, :],
                start=True,
                stop=True,
            )
            if c % 2 == 0:
                nc.scalar.activation(a[:, cols], acc[:], COPY)
            else:
                nc.vector.tensor_copy(out=a[:, cols], in_=acc[:])

        n_part = T // N_MX
        per_part = N_MX // P
        down = [ps.tile([P, N_MX], F32, name=f"down{b}") for b in range(n_part)]
        for b in range(n_part):
            for j in range(per_part):
                nc.tensor.matmul(
                    down[b][:, j * P : (j + 1) * P],
                    lhsT=old_sb[:, b * N_MX + j * P : b * N_MX + (j + 1) * P],
                    rhs=ident[:],
                    is_transpose=True,
                    start=(j == 0),
                    stop=False,
                )

        s0, s1 = slice(0, HALF), slice(HALF, I)
        l0, l1 = slice(0, HALF // 16), slice(HALF // 16, I // 16)
        halves = ((s0, l0), (s1, l1))
        for s, l in halves:
            nc.scalar.activation(ng2[:, s], a[:].indirect(list2[:, l]), COPY, scale=-1.0)
            nc.vector.tensor_copy(g1[:, s], a[:].indirect(list1[:, l]))
        for s, l in halves:
            nc.vector.scalar_tensor_tensor(top[:, s], ng2[:, s], -1.0, g1[:, s], MULT, MAX)
        for h, (s, l) in enumerate(halves):
            nc.vector.tensor_tensor(f1[h][:].indirect(list1[:, l]), top[:, s], ng2[:, s], ADD)
        nc.vector.tensor_tensor(f2[:].indirect(list3[:]), top[:], ng2[:], ADD)

        for b in range(n_part):
            for j in range(per_part):
                nc.tensor.matmul(
                    down[b][:, j * P : (j + 1) * P],
                    lhsT=f1[0][:, b * N_MX + j * P : b * N_MX + (j + 1) * P],
                    rhs=ident[:],
                    is_transpose=True,
                    start=False,
                    stop=False,
                )

        back = [ps.tile([P, N_MX], F32, name=f"acc{b}") for b in range(n_part)]

        def turn_down(b):
            for j in range(per_part):
                nc.tensor.matmul(
                    down[b][:, j * P : (j + 1) * P],
                    lhsT=f1[1][:, b * N_MX + j * P : b * N_MX + (j + 1) * P],
                    rhs=ident[:],
                    is_transpose=True,
                    start=False,
                    stop=(j == per_part - 1),
                )
            nc.scalar.copy(turned[:, b * N_MX : (b + 1) * N_MX], down[b][:])

        def turn_back(b):
            for j in range(per_part):
                nc.tensor.transpose(
                    back[b][:, j * P : (j + 1) * P],
                    turned[:, b * N_MX + j * P : b * N_MX + (j + 1) * P],
                    ident[:],
                )

        for b in range(n_part + 2):
            if b < n_part:
                turn_down(b)
            if b >= 2:
                turn_back(b - 2)

        for c in range(n_part):
            cols = slice(c * N_MX, (c + 1) * N_MX)
            nc.vector.scalar_tensor_tensor(res[:, cols], f2[:, cols], share_sb[:, 0:1], back[c][:], MULT, ADD)
            queue = nc.sync if c % 2 == 0 else nc.scalar
            queue.dma_start(out=out[:, cols], in_=res[:, cols])
